import numpy as np, ml_dtypes
CORES = [24,25,26,27,28,29,30,31,224,225,226,227,228,229,230,231]
N = 16
KB, QP, ROOT = 1, 512, 9
def setup_inputs(rng):
    return {"q": rng.standard_normal((N, 128, QP), dtype=np.float32).astype(ml_dtypes.bfloat16), "k": rng.standard_normal((N, 128, KB * 128), dtype=np.float32).astype(ml_dtypes.bfloat16), "v": rng.standard_normal((N, 128, KB * 128), dtype=np.float32).astype(ml_dtypes.bfloat16)}
def setup_inputs_big(rng):
    d = setup_inputs(rng)
    for k in ("q", "k", "v"): d[k] = (d[k].astype(np.float32) * 1024.0).astype(d[k].dtype)
    return d
def setup_inputs_small(rng):
    d = setup_inputs(rng)
    for k in ("q", "k", "v"): d[k] = (d[k].astype(np.float32) * (1 / 1024.0)).astype(d[k].dtype)
    return d
def setup_inputs_apart(rng):
    d = setup_inputs(rng)
    f = (10.0 ** rng.permutation(np.linspace(-1.5, 1.5, N))).astype(np.float32).reshape(N, 1, 1)
    for k in ("q", "k", "v"): d[k] = (d[k].astype(np.float32) * f).astype(d[k].dtype)
    return d
def reference(q, k, v):
    Q, K, V = q.astype(np.float64), k.astype(np.float64), v.astype(np.float64)
    o = np.zeros((128, QP))
    for j in range(N):
        for b in range(KB):
            o += V[j][:, 128 * b:128 * b + 128].T @ np.maximum(K[j][:, 128 * b:128 * b + 128].T @ Q[ROOT], 0.0)
    y = np.full((N, 128, QP), np.nan)
    y[ROOT] = o
    return {"y": y.astype(ml_dtypes.bfloat16 if q.dtype != np.float64 else np.float64)}

@@ -1,0 +1,208 @@
+from concourse.bass import DstId, RemoteDMATransfer
+from concourse.mybir import AluOpType
+
+KP = 128
+W = 256
+NSLOT = 6
+NKV = 8
+LOOK = 2
+E_ALL = 16
+E_HAND = 8
+
+SCRATCH = {
+    "qs": ("sbuf", [128, 2 * W], "bfloat16"),
+    "kv": ("sbuf", [128, 2 * KP], "bfloat16"),
+    "kvin": ("sbuf", [128, NKV * 2 * KP], "bfloat16"),
+    "zero": ("sbuf", [128, W], "float32"),
+    "s": ("sbuf", [128, NSLOT * W], "bfloat16"),
+    "osb": ("sbuf", [128, 2 * W], "bfloat16"),
+    "oland": ("sbuf", [128, 2 * W], "bfloat16"),
+    "ps_o0": ("psum", [128, 512], "float32"),
+    "ps_o1": ("psum", [128, 512], "float32"),
+}
+for _i in range(NSLOT):
+    SCRATCH["ps_s%d" % _i] = ("psum", [128, 512], "float32")
+
+SEMAPHORES = ["ld", "qin", "zr", "snd", "st", "cp0", "cp1", "pa0", "pa1"]
+SEMAPHORES += ["kva%d" % _i for _i in range(NKV)]
+for _n in ("m1", "rl", "m2"):
+    SEMAPHORES += ["%s_%d" % (_n, _i) for _i in range(NSLOT)]
+
+
+def same_chip(topo, a, b):
+    return topo.host(a) == topo.host(b) and topo.chip(a) == topo.chip(b)
+
+
+def pick(mask, n, skip=0):
+    bits = [b for b in range(mask.bit_length()) if (mask >> b) & 1]
+    m = 0
+    for b in bits[skip:skip + n]:
+        m |= 1 << b
+    return m
+
+
+def count(mask):
+    return sum((mask >> b) & 1 for b in range(mask.bit_length()))
+
+
+def layout(T, topo):
+    cores = list(T.cores)
+    root = cores[T.root]
+    near = [c for c in cores if c != root and same_chip(topo, c, root)]
+    far = [c for c in cores if not same_chip(topo, c, root)]
+    direct = [c for c in far if topo.may_write(c, root)]
+    late = [c for c in far if not topo.may_write(c, root)]
+    fwd, load = {}, {d: 0 for d in direct}
+    for c in late:
+        d = sorted(direct, key=lambda x: (load[x], topo.die(x) != topo.die(c), x))[0]
+        fwd[c] = d
+        load[d] += 1
+    near = sorted(near, key=lambda c: (topo.die(c) != topo.die(root), c))
+    return root, near, near[:2], direct, late, fwd
+
+
+def kv_slot(T, s):
+    return T.kvin[:, s * 2 * KP:(s + 1) * 2 * KP]
+
+
+def unit(T, s, half, waits, grp):
+    if s is None:
+        k, v = T.kv[:, 0:KP], T.kv[:, KP:2 * KP]
+    else:
+        k, v = T.kvin[:, s * 2 * KP:s * 2 * KP + KP], T.kvin[:, s * 2 * KP + KP:(s + 1) * 2 * KP]
+    return {"k": k, "v": v, "half": half, "waits": waits, "grp": grp}
+
+
+def compute(g, T, units, qval, vadd):
+    te, ve = g.tensor, g.vector
+    n = len(units)
+    first, last = {}, {}
+    for u, b in enumerate(units):
+        first.setdefault(b["half"], u)
+        last[b["half"]] = u
+    ve.memset(T.zero[:], 0.0).then_inc(T.sem.zr, 1)
+    ve.wait_ge(T.sem.zr, 1)
+    te.wait_ge(T.sem.qin, qval)
+
+    def mm1(u):
+        b, s, r = units[u], u % NSLOT, u // NSLOT
+        h = b["half"]
+        for sem, val in b["waits"]:
+            te.wait_ge(sem, val)
+        ps = T["ps_s%d" % s][:, 0:W]
+        te.matmul(ps, b["k"], T.qs[:, h * W:(h + 1) * W], True, True).then_inc(T.sem["m1_%d" % s], 1)
+        ve.wait_ge(T.sem["m1_%d" % s], r + 1)
+        if r > 0:
+            ve.wait_ge(T.sem["m2_%d" % s], r)
+        ve.tensor_tensor(T.s[:, s * W:(s + 1) * W], ps, T.zero[:], AluOpType.max).then_inc(T.sem["rl_%d" % s], 1)
+
+    done = 0
+    for u, b in enumerate(units):
+        lim = u
+        while lim + 1 < n and lim + 1 <= u + LOOK and units[lim + 1]["grp"] == b["grp"]:
+            lim += 1
+        while done <= lim:
+            mm1(done)
+            done += 1
+        s, h = u % NSLOT, b["half"]
+        te.wait_ge(T.sem["rl_%d" % s], u // NSLOT + 1)
+        te.matmul(T["ps_o%d" % h][:, 0:W], b["v"], T.s[:, s * W:(s + 1) * W],
+                  u == first[h], u == last[h]).then_inc(T.sem["m2_%d" % s], 1)
+
+    for h in sorted(last, key=lambda x: last[x]):
+        for s in range(NSLOT):
+            us = [u for u in range(n) if units[u]["half"] == h and u % NSLOT == s]
+            if us:
+                ve.wait_ge(T.sem["m2_%d" % s], max(us) // NSLOT + 1)
+        out, acc = T.osb[:, h * W:(h + 1) * W], T["ps_o%d" % h][:, 0:W]
+        if h in vadd:
+            ap, waits = vadd[h]
+            for sem, val in waits:
+                ve.wait_ge(sem, val)
+            ve.tensor_tensor(out, acc, ap, AluOpType.add).then_inc(T.sem["cp%d" % h], 1)
+        else:
+            ve.tensor_copy(out, acc).then_inc(T.sem["cp%d" % h], 1)
+
+
+def send(g, T, topo, core, dst, out_ap, in_ap, sem, n):
+    rid, pid = topo.addr(dst, core)
+    m = pick(topo.mask(core, dst), n)
+    g.remote_dma(out_ap=out_ap, in_ap=in_ap, remote_sem=sem, local_sem=T.sem.snd, pid=pid, routing_id=rid,
+                 dma_engine_mask=m)
+    return count(m)
+
+
+def dst_id(topo, dst, core):
+    rid, pid = topo.addr(dst, core)
+    return DstId(rid=rid, pnc=pid)
+
+
+def rank_program(g, core, T, topo):
+    if T.rank_of(core) is None:
+        return
+    root, near, pair, direct, late, fwd = layout(T, topo)
+    e_on = count(pick(topo.mask(pair[0], root), E_ALL))
+    e_off = count(pick(topo.mask(direct[0], root), E_ALL))
+    e_q = e_on // 2
+
+    if core == root:
+        g.sync.dma_start(T.qs[:], T.q[:]).then_inc(T.sem.qin, 16)
+    g.scalar.dma_start(T.kv[:, 0:KP], T.k[:]).then_inc(T.sem.ld, 16)
+    g.sync.dma_start(T.kv[:, KP:2 * KP], T.v[:]).then_inc(T.sem.ld, 16)
+    own = [(T.sem.ld, 32)]
+
+    if core == root:
+        g.wait_ge(T.sem.qin, 16)
+        trs = []
+        for h, p in enumerate(pair):
+            ap = T.qs[:, h * W:(h + 1) * W]
+            trs.append(RemoteDMATransfer(dst_ids=[dst_id(topo, p, core)],
+                                         dma_engine_mask=pick(topo.mask(core, p), e_q, h * e_q),
+                                         remote_sem=T.sem.qin, src=ap, dst=ap))
+        g.remote_dma_fused(trs, local_sem=T.sem.snd)
+        units = [unit(T, None, h, own, 0) for h in range(2)]
+        for i in range(len(direct) + len(late)):
+            grp = 1 if i < len(direct) else 2
+            units += [unit(T, i, h, [(T.sem["kva%d" % i], e_off)], grp) for h in range(2)]
+        vadd = {h: (T.oland[:, h * W:(h + 1) * W], [(T.sem["pa%d" % h], e_on)]) for h in range(2)}
+        compute(g, T, units, 16, vadd)
+        for h, qu in enumerate((g.sync, g.scalar)):
+            qu.wait_ge(T.sem["cp%d" % h], 1)
+            qu.dma_start(T.y[:, h * W:(h + 1) * W], T.osb[:, h * W:(h + 1) * W]).then_inc(T.sem.st, 16)
+        g.wait_ge(T.sem.snd, 2 * e_q)
+        g.wait_ge(T.sem.st, 32)
+        return
+
+    g.wait_ge(T.sem.ld, 32)
+    sent = 0
+    if core in pair:
+        h = pair.index(core)
+        mate = pair[1 - h]
+        me = near.index(core)
+        sent += send(g, T, topo, core, mate, kv_slot(T, me), T.kv[:], T.sem["kva%d" % me], E_ALL)
+        units = [unit(T, None, h, own, 0)]
+        order = [near.index(mate)] + [i for i, c in enumerate(near) if c not in pair]
+        units += [unit(T, i, h, [(T.sem["kva%d" % i], e_on)], 0) for i in order]
+        compute(g, T, units, e_q, {})
+        g.wait_ge(T.sem["cp%d" % h], 1)
+        ap = T.osb[:, h * W:(h + 1) * W]
+        sent += send(g, T, topo, core, root, T.oland[:, h * W:(h + 1) * W], ap, T.sem["pa%d" % h], E_ALL)
+    elif core in near:
+        me = near.index(core)
+        m = pick(topo.mask(core, pair[0]) & topo.mask(core, pair[1]), E_ALL)
+        g.remote_dma_fused([RemoteDMATransfer(dst_ids=[dst_id(topo, p, core) for p in pair], dma_engine_mask=m,
+                                              remote_sem=T.sem["kva%d" % me], srcs=[T.kv[:]],
+                                              dsts=[kv_slot(T, me) for p in pair])], local_sem=T.sem.snd)
+        sent += count(m)
+    elif core in direct:
+        i = direct.index(core)
+        sent += send(g, T, topo, core, root, kv_slot(T, i), T.kv[:], T.sem["kva%d" % i], E_ALL)
+        for n, c in enumerate([c for c in late if fwd[c] == core]):
+            g.wait_ge(T.sem["kva%d" % n], count(pick(topo.mask(c, core), E_HAND)))
+            j = len(direct) + late.index(c)
+            sent += send(g, T, topo, core, root, kv_slot(T, j), kv_slot(T, n), T.sem["kva%d" % j], E_ALL)
+    else:
+        d = fwd[core]
+        n = [c for c in late if fwd[c] == d].index(core)
+        sent += send(g, T, topo, core, d, kv_slot(T, n), T.kv[:], T.sem["kva%d" % n], E_HAND)
+    g.wait_ge(T.sem.snd, sent)

@@ -4,10 +4,12 @@ from concourse.mybir import AluOpType
 KP = 128
 W = 256
 NSLOT = 6
-NKV = 8
+NKV = 9
 LOOK = 2
 E_ALL = 16
 E_HAND = 8
+ND = 1
+LAST = True
 
 SCRATCH = {
     "qs": ("sbuf", [128, 2 * W], "bfloat16"),
@@ -45,20 +47,35 @@ def count(mask):
     return sum((mask >> b) & 1 for b in range(mask.bit_length()))
 
 
+def assign(topo, owners, passers, fwd):
+    load = {d: 0 for d in passers}
+    for c in owners:
+        ok = [r for r in passers if topo.may_write(c, r)]
+        d = sorted(ok, key=lambda x: (load[x], topo.die(x) != topo.die(c), x))[0]
+        fwd[c] = d
+        load[d] += 1
+
+
 def layout(T, topo):
     cores = list(T.cores)
     root = cores[T.root]
     near = [c for c in cores if c != root and same_chip(topo, c, root)]
+    near = sorted(near, key=lambda c: (topo.die(c) != topo.die(root), c))
+    pair = near[:2]
     far = [c for c in cores if not same_chip(topo, c, root)]
     direct = [c for c in far if topo.may_write(c, root)]
     late = [c for c in far if not topo.may_write(c, root)]
-    fwd, load = {}, {d: 0 for d in direct}
-    for c in late:
-        d = sorted(direct, key=lambda x: (load[x], topo.die(x) != topo.die(c), x))[0]
-        fwd[c] = d
-        load[d] += 1
-    near = sorted(near, key=lambda c: (topo.die(c) != topo.die(root), c))
-    return root, near, near[:2], direct, late, fwd
+    fwd = {}
+    assign(topo, late, direct, fwd)
+    dies = sorted({topo.die(c) for c in direct}, key=lambda d: d == topo.die(root))
+    turn = [[c for c in direct if topo.die(c) == d] for d in dies]
+    if LAST:
+        turn = [t[::-1] for t in turn]
+    topair = [t[i] for i in range(len(direct)) for t in turn if i < len(t)][:ND]
+    world = range((max(topo.host(c) for c in cores) + 1) * topo.CORES_PER_HOST)
+    outside = [r for r in world if r not in cores and topo.mates(r, root) and topo.may_write(r, root)]
+    assign(topo, [c for c in late if fwd[c] in topair], outside, fwd)
+    return root, near, pair, direct, late, fwd, topair
 
 
 def kv_slot(T, s):
@@ -137,13 +154,33 @@ def dst_id(topo, dst, core):
     return DstId(rid=rid, pnc=pid)
 
 
+def to_pair(g, T, topo, core, pair, s):
+    m = pick(topo.mask(core, pair[0]) & topo.mask(core, pair[1]), E_ALL)
+    g.remote_dma_fused([RemoteDMATransfer(dst_ids=[dst_id(topo, p, core) for p in pair], dma_engine_mask=m,
+                                          remote_sem=T.sem["kva%d" % s], srcs=[T.kv[:]],
+                                          dsts=[kv_slot(T, s) for p in pair])], local_sem=T.sem.snd)
+    return count(m)
+
+
+def pass_on(g, T, topo, core, root, direct, late, fwd):
+    sent = 0
+    for n, c in enumerate([c for c in late if fwd[c] == core]):
+        g.wait_ge(T.sem["kva%d" % n], count(pick(topo.mask(c, core), E_HAND)))
+        j = len(direct) + late.index(c)
+        sent += send(g, T, topo, core, root, kv_slot(T, j), kv_slot(T, n), T.sem["kva%d" % j], E_ALL)
+    return sent
+
+
 def rank_program(g, core, T, topo):
+    root, near, pair, direct, late, fwd, topair = layout(T, topo)
     if T.rank_of(core) is None:
+        if core in fwd.values():
+            g.wait_ge(T.sem.snd, pass_on(g, T, topo, core, root, direct, late, fwd))
         return
-    root, near, pair, direct, late, fwd = layout(T, topo)
     e_on = count(pick(topo.mask(pair[0], root), E_ALL))
     e_off = count(pick(topo.mask(direct[0], root), E_ALL))
     e_q = e_on // 2
+    nfar = len(direct) + len(late)
 
     if core == root:
         g.sync.dma_start(T.qs[:], T.q[:]).then_inc(T.sem.qin, 16)
@@ -161,8 +198,12 @@ def rank_program(g, core, T, topo):
                                          remote_sem=T.sem.qin, src=ap, dst=ap))
         g.remote_dma_fused(trs, local_sem=T.sem.snd)
         units = [unit(T, None, h, own, 0) for h in range(2)]
-        for i in range(len(direct) + len(late)):
-            grp = 1 if i < len(direct) else 2
+        seq = list(range(len(direct)))
+        seq += sorted(range(len(direct), nfar), key=lambda j: fwd[late[j - len(direct)]] not in direct)
+        for i in seq:
+            if i < len(direct) and direct[i] in topair:
+                continue
+            grp = 2 if i >= len(direct) else 1
             units += [unit(T, i, h, [(T.sem["kva%d" % i], e_off)], grp) for h in range(2)]
         vadd = {h: (T.oland[:, h * W:(h + 1) * W], [(T.sem["pa%d" % h], e_on)]) for h in range(2)}
         compute(g, T, units, 16, vadd)
@@ -183,24 +224,20 @@ def rank_program(g, core, T, topo):
         units = [unit(T, None, h, own, 0)]
         order = [near.index(mate)] + [i for i, c in enumerate(near) if c not in pair]
         units += [unit(T, i, h, [(T.sem["kva%d" % i], e_on)], 0) for i in order]
+        units += [unit(T, len(near) + i, h, [(T.sem["kva%d" % (len(near) + i)], e_off)], 0) for i in range(ND)]
         compute(g, T, units, e_q, {})
         g.wait_ge(T.sem["cp%d" % h], 1)
         ap = T.osb[:, h * W:(h + 1) * W]
         sent += send(g, T, topo, core, root, T.oland[:, h * W:(h + 1) * W], ap, T.sem["pa%d" % h], E_ALL)
     elif core in near:
-        me = near.index(core)
-        m = pick(topo.mask(core, pair[0]) & topo.mask(core, pair[1]), E_ALL)
-        g.remote_dma_fused([RemoteDMATransfer(dst_ids=[dst_id(topo, p, core) for p in pair], dma_engine_mask=m,
-                                              remote_sem=T.sem["kva%d" % me], srcs=[T.kv[:]],
-                                              dsts=[kv_slot(T, me) for p in pair])], local_sem=T.sem.snd)
-        sent += count(m)
+        sent += to_pair(g, T, topo, core, pair, near.index(core))
     elif core in direct:
-        i = direct.index(core)
-        sent += send(g, T, topo, core, root, kv_slot(T, i), T.kv[:], T.sem["kva%d" % i], E_ALL)
-        for n, c in enumerate([c for c in late if fwd[c] == core]):
-            g.wait_ge(T.sem["kva%d" % n], count(pick(topo.mask(c, core), E_HAND)))
-            j = len(direct) + late.index(c)
-            sent += send(g, T, topo, core, root, kv_slot(T, j), kv_slot(T, n), T.sem["kva%d" % j], E_ALL)
+        if core in topair:
+            sent += to_pair(g, T, topo, core, pair, len(near) + topair.index(core))
+        else:
+            i = direct.index(core)
+            sent += send(g, T, topo, core, root, kv_slot(T, i), T.kv[:], T.sem["kva%d" % i], E_ALL)
+        sent += pass_on(g, T, topo, core, root, direct, late, fwd)
     else:
         d = fwd[core]
         n = [c for c in late if fwd[c] == d].index(core)

@@ -6,6 +6,7 @@ W = 256
 NSLOT = 6
 NKV = 9
 LOOK = 2
+LOOK_ROOT = 4
 E_ALL = 16
 E_HAND = 8
 ND = 1
@@ -90,7 +91,7 @@ def unit(T, s, half, waits, grp):
     return {"k": k, "v": v, "half": half, "waits": waits, "grp": grp}
 
 
-def compute(g, T, units, qval, vadd):
+def compute(g, T, units, qval, vadd, look):
     te, ve = g.tensor, g.vector
     n = len(units)
     first, last = {}, {}
@@ -116,7 +117,7 @@ def compute(g, T, units, qval, vadd):
     done = 0
     for u, b in enumerate(units):
         lim = u
-        while lim + 1 < n and lim + 1 <= u + LOOK and units[lim + 1]["grp"] == b["grp"]:
+        while lim + 1 < n and lim + 1 <= u + look and units[lim + 1]["grp"] == b["grp"]:
             lim += 1
         while done <= lim:
             mm1(done)
@@ -206,7 +207,7 @@ def rank_program(g, core, T, topo):
             grp = 2 if i >= len(direct) else 1
             units += [unit(T, i, h, [(T.sem["kva%d" % i], e_off)], grp) for h in range(2)]
         vadd = {h: (T.oland[:, h * W:(h + 1) * W], [(T.sem["pa%d" % h], e_on)]) for h in range(2)}
-        compute(g, T, units, 16, vadd)
+        compute(g, T, units, 16, vadd, LOOK_ROOT)
         for h, qu in enumerate((g.sync, g.scalar)):
             qu.wait_ge(T.sem["cp%d" % h], 1)
             qu.dma_start(T.y[:, h * W:(h + 1) * W], T.osb[:, h * W:(h + 1) * W]).then_inc(T.sem.st, 16)
@@ -225,7 +226,7 @@ def rank_program(g, core, T, topo):
         order = [near.index(mate)] + [i for i, c in enumerate(near) if c not in pair]
         units += [unit(T, i, h, [(T.sem["kva%d" % i], e_on)], 0) for i in order]
         units += [unit(T, len(near) + i, h, [(T.sem["kva%d" % (len(near) + i)], e_off)], 0) for i in range(ND)]
-        compute(g, T, units, e_q, {})
+        compute(g, T, units, e_q, {}, LOOK)
         g.wait_ge(T.sem["cp%d" % h], 1)
         ap = T.osb[:, h * W:(h + 1) * W]
         sent += send(g, T, topo, core, root, T.oland[:, h * W:(h + 1) * W], ap, T.sem["pa%d" % h], E_ALL)

from concourse.bass import DstId, RemoteDMATransfer
from concourse.mybir import AluOpType

KP = 128
W = 256
NSLOT = 6
NKV = 9
LOOK = 2
LOOK_ROOT = 4
E_ALL = 16
E_HAND = 8
ND = 1
LAST = True

SCRATCH = {
    "qs": ("sbuf", [128, 2 * W], "bfloat16"),
    "kv": ("sbuf", [128, 2 * KP], "bfloat16"),
    "kvin": ("sbuf", [128, NKV * 2 * KP], "bfloat16"),
    "zero": ("sbuf", [128, W], "float32"),
    "s": ("sbuf", [128, NSLOT * W], "bfloat16"),
    "osb": ("sbuf", [128, 2 * W], "bfloat16"),
    "oland": ("sbuf", [128, 2 * W], "bfloat16"),
    "ps_o0": ("psum", [128, 512], "float32"),
    "ps_o1": ("psum", [128, 512], "float32"),
}
for _i in range(NSLOT):
    SCRATCH["ps_s%d" % _i] = ("psum", [128, 512], "float32")

SEMAPHORES = ["ld", "qin", "zr", "snd", "st", "cp0", "cp1", "pa0", "pa1"]
SEMAPHORES += ["kva%d" % _i for _i in range(NKV)]
for _n in ("m1", "rl", "m2"):
    SEMAPHORES += ["%s_%d" % (_n, _i) for _i in range(NSLOT)]


def same_chip(topo, a, b):
    return topo.host(a) == topo.host(b) and topo.chip(a) == topo.chip(b)


def pick(mask, n, skip=0):
    bits = [b for b in range(mask.bit_length()) if (mask >> b) & 1]
    m = 0
    for b in bits[skip:skip + n]:
        m |= 1 << b
    return m


def count(mask):
    return sum((mask >> b) & 1 for b in range(mask.bit_length()))


def assign(topo, owners, passers, fwd):
    load = {d: 0 for d in passers}
    for c in owners:
        ok = [r for r in passers if topo.may_write(c, r)]
        d = sorted(ok, key=lambda x: (load[x], topo.die(x) != topo.die(c), x))[0]
        fwd[c] = d
        load[d] += 1


def layout(T, topo):
    cores = list(T.cores)
    root = cores[T.root]
    near = [c for c in cores if c != root and same_chip(topo, c, root)]
    near = sorted(near, key=lambda c: (topo.die(c) != topo.die(root), c))
    pair = near[:2]
    far = [c for c in cores if not same_chip(topo, c, root)]
    direct = [c for c in far if topo.may_write(c, root)]
    late = [c for c in far if not topo.may_write(c, root)]
    fwd = {}
    assign(topo, late, direct, fwd)
    dies = sorted({topo.die(c) for c in direct}, key=lambda d: d == topo.die(root))
    turn = [[c for c in direct if topo.die(c) == d] for d in dies]
    if LAST:
        turn = [t[::-1] for t in turn]
    topair = [t[i] for i in range(len(direct)) for t in turn if i < len(t)][:ND]
    world = range((max(topo.host(c) for c in cores) + 1) * topo.CORES_PER_HOST)
    outside = [r for r in world if r not in cores and topo.mates(r, root) and topo.may_write(r, root)]
    assign(topo, [c for c in late if fwd[c] in topair], outside, fwd)
    return root, near, pair, direct, late, fwd, topair


def kv_slot(T, s):
    return T.kvin[:, s * 2 * KP:(s + 1) * 2 * KP]


def unit(T, s, half, waits, grp):
    if s is None:
        k, v = T.kv[:, 0:KP], T.kv[:, KP:2 * KP]
    else:
        k, v = T.kvin[:, s * 2 * KP:s * 2 * KP + KP], T.kvin[:, s * 2 * KP + KP:(s + 1) * 2 * KP]
    return {"k": k, "v": v, "half": half, "waits": waits, "grp": grp}


def compute(g, T, units, qval, vadd, look):
    te, ve = g.tensor, g.vector
    n = len(units)
    first, last = {}, {}
    for u, b in enumerate(units):
        first.setdefault(b["half"], u)
        last[b["half"]] = u
    ve.memset(T.zero[:], 0.0).then_inc(T.sem.zr, 1)
    ve.wait_ge(T.sem.zr, 1)
    te.wait_ge(T.sem.qin, qval)

    def mm1(u):
        b, s, r = units[u], u % NSLOT, u // NSLOT
        h = b["half"]
        for sem, val in b["waits"]:
            te.wait_ge(sem, val)
        ps = T["ps_s%d" % s][:, 0:W]
        te.matmul(ps, b["k"], T.qs[:, h * W:(h + 1) * W], True, True).then_inc(T.sem["m1_%d" % s], 1)
        ve.wait_ge(T.sem["m1_%d" % s], r + 1)
        if r > 0:
            ve.wait_ge(T.sem["m2_%d" % s], r)
        ve.tensor_tensor(T.s[:, s * W:(s + 1) * W], ps, T.zero[:], AluOpType.max).then_inc(T.sem["rl_%d" % s], 1)

    done = 0
    for u, b in enumerate(units):
        lim = u
        while lim + 1 < n and lim + 1 <= u + look and units[lim + 1]["grp"] == b["grp"]:
            lim += 1
        while done <= lim:
            mm1(done)
            done += 1
        s, h = u % NSLOT, b["half"]
        te.wait_ge(T.sem["rl_%d" % s], u // NSLOT + 1)
        te.matmul(T["ps_o%d" % h][:, 0:W], b["v"], T.s[:, s * W:(s + 1) * W],
                  u == first[h], u == last[h]).then_inc(T.sem["m2_%d" % s], 1)

    for h in sorted(last, key=lambda x: last[x]):
        for s in range(NSLOT):
            us = [u for u in range(n) if units[u]["half"] == h and u % NSLOT == s]
            if us:
                ve.wait_ge(T.sem["m2_%d" % s], max(us) // NSLOT + 1)
        out, acc = T.osb[:, h * W:(h + 1) * W], T["ps_o%d" % h][:, 0:W]
        if h in vadd:
            ap, waits = vadd[h]
            for sem, val in waits:
                ve.wait_ge(sem, val)
            ve.tensor_tensor(out, acc, ap, AluOpType.add).then_inc(T.sem["cp%d" % h], 1)
        else:
            ve.tensor_copy(out, acc).then_inc(T.sem["cp%d" % h], 1)


def send(g, T, topo, core, dst, out_ap, in_ap, sem, n):
    rid, pid = topo.addr(dst, core)
    m = pick(topo.mask(core, dst), n)
    g.remote_dma(out_ap=out_ap, in_ap=in_ap, remote_sem=sem, local_sem=T.sem.snd, pid=pid, routing_id=rid,
                 dma_engine_mask=m)
    return count(m)


def dst_id(topo, dst, core):
    rid, pid = topo.addr(dst, core)
    return DstId(rid=rid, pnc=pid)


def to_pair(g, T, topo, core, pair, s):
    m = pick(topo.mask(core, pair[0]) & topo.mask(core, pair[1]), E_ALL)
    g.remote_dma_fused([RemoteDMATransfer(dst_ids=[dst_id(topo, p, core) for p in pair], dma_engine_mask=m,
                                          remote_sem=T.sem["kva%d" % s], srcs=[T.kv[:]],
                                          dsts=[kv_slot(T, s) for p in pair])], local_sem=T.sem.snd)
    return count(m)


def pass_on(g, T, topo, core, root, direct, late, fwd):
    sent = 0
    for n, c in enumerate([c for c in late if fwd[c] == core]):
        g.wait_ge(T.sem["kva%d" % n], count(pick(topo.mask(c, core), E_HAND)))
        j = len(direct) + late.index(c)
        sent += send(g, T, topo, core, root, kv_slot(T, j), kv_slot(T, n), T.sem["kva%d" % j], E_ALL)
    return sent


def rank_program(g, core, T, topo):
    root, near, pair, direct, late, fwd, topair = layout(T, topo)
    if T.rank_of(core) is None:
        if core in fwd.values():
            g.wait_ge(T.sem.snd, pass_on(g, T, topo, core, root, direct, late, fwd))
        return
    e_on = count(pick(topo.mask(pair[0], root), E_ALL))
    e_off = count(pick(topo.mask(direct[0], root), E_ALL))
    e_q = e_on // 2
    nfar = len(direct) + len(late)

    if core == root:
        g.sync.dma_start(T.qs[:], T.q[:]).then_inc(T.sem.qin, 16)
    g.scalar.dma_start(T.kv[:, 0:KP], T.k[:]).then_inc(T.sem.ld, 16)
    g.sync.dma_start(T.kv[:, KP:2 * KP], T.v[:]).then_inc(T.sem.ld, 16)
    own = [(T.sem.ld, 32)]

    if core == root:
        g.wait_ge(T.sem.qin, 16)
        trs = []
        for h, p in enumerate(pair):
            ap = T.qs[:, h * W:(h + 1) * W]
            trs.append(RemoteDMATransfer(dst_ids=[dst_id(topo, p, core)],
                                         dma_engine_mask=pick(topo.mask(core, p), e_q, h * e_q),
                                         remote_sem=T.sem.qin, src=ap, dst=ap))
        g.remote_dma_fused(trs, local_sem=T.sem.snd)
        units = [unit(T, None, h, own, 0) for h in range(2)]
        seq = list(range(len(direct)))
        seq += sorted(range(len(direct), nfar), key=lambda j: fwd[late[j - len(direct)]] not in direct)
        for i in seq:
            if i < len(direct) and direct[i] in topair:
                continue
            grp = 2 if i >= len(direct) else 1
            units += [unit(T, i, h, [(T.sem["kva%d" % i], e_off)], grp) for h in range(2)]
        vadd = {h: (T.oland[:, h * W:(h + 1) * W], [(T.sem["pa%d" % h], e_on)]) for h in range(2)}
        compute(g, T, units, 16, vadd, LOOK_ROOT)
        for h, qu in enumerate((g.sync, g.scalar)):
            qu.wait_ge(T.sem["cp%d" % h], 1)
            qu.dma_start(T.y[:, h * W:(h + 1) * W], T.osb[:, h * W:(h + 1) * W]).then_inc(T.sem.st, 16)
        g.wait_ge(T.sem.snd, 2 * e_q)
        g.wait_ge(T.sem.st, 32)
        return

    g.wait_ge(T.sem.ld, 32)
    sent = 0
    if core in pair:
        h = pair.index(core)
        mate = pair[1 - h]
        me = near.index(core)
        sent += send(g, T, topo, core, mate, kv_slot(T, me), T.kv[:], T.sem["kva%d" % me], E_ALL)
        units = [unit(T, None, h, own, 0)]
        order = [near.index(mate)] + [i for i, c in enumerate(near) if c not in pair]
        units += [unit(T, i, h, [(T.sem["kva%d" % i], e_on)], 0) for i in order]
        units += [unit(T, len(near) + i, h, [(T.sem["kva%d" % (len(near) + i)], e_off)], 0) for i in range(ND)]
        compute(g, T, units, e_q, {}, LOOK)
        g.wait_ge(T.sem["cp%d" % h], 1)
        ap = T.osb[:, h * W:(h + 1) * W]
        sent += send(g, T, topo, core, root, T.oland[:, h * W:(h + 1) * W], ap, T.sem["pa%d" % h], E_ALL)
    elif core in near:
        sent += to_pair(g, T, topo, core, pair, near.index(core))
    elif core in direct:
        if core in topair:
            sent += to_pair(g, T, topo, core, pair, len(near) + topair.index(core))
        else:
            i = direct.index(core)
            sent += send(g, T, topo, core, root, kv_slot(T, i), T.kv[:], T.sem["kva%d" % i], E_ALL)
        sent += pass_on(g, T, topo, core, root, direct, late, fwd)
    else:
        d = fwd[core]
        n = [c for c in late if fwd[c] == d].index(core)
        sent += send(g, T, topo, core, d, kv_slot(T, n), T.kv[:], T.sem["kva%d" % n], E_HAND)
    g.wait_ge(T.sem.snd, sent)
